import numpy as np
import ml_dtypes


def mxq(x, axis, fmt="e4m3"):
    dtype, down = {"e4m3": (ml_dtypes.float8_e4m3fn, 7), "e5m2": (ml_dtypes.float8_e5m2, 14)}[fmt]
    v = np.moveaxis(np.asarray(x, np.float32).astype(ml_dtypes.bfloat16).astype(np.float64), axis, -1)
    blocks = v.reshape(v.shape[:-1] + (-1, 32))
    amax = np.abs(blocks).max(-1, keepdims=True)
    byte = np.maximum(np.where(amax > 0, np.frexp(amax)[1] - 1 + 127, 0) - down, 1)
    scale = np.exp2(byte - 127.0)
    codes = (blocks / scale).astype(np.float32).astype(dtype).astype(np.float64)
    return np.moveaxis((codes * scale).reshape(v.shape), -1, axis)


WIDE = False


def mx_kscale(k):
    if not WIDE:
        return np.ones(k)
    levels = np.array([10, -10, 5, -5, 0])
    if k % 512:
        return np.exp2(np.random.permutation(np.resize(levels, k // 32))).repeat(32)
    a = np.empty((k // 512, 16))
    for p in range(k // 512):
        a[p, :8] = np.random.permutation(np.resize(levels, 8))
        for g in range(8):
            far = levels[np.abs(levels - a[p, g]) >= 10]
            a[p, g + 8] = far[np.random.randint(len(far))]
    return np.exp2(a.ravel()).repeat(32)


def f64(x):
    return np.asarray(x).astype(np.float64)


def striped(idx):
    return np.tile(idx.reshape(-1, 16).T, (8, 1)).astype(np.uint16)


def unstriped(offs):
    return offs[:16].T.reshape(-1).astype(np.int64)


def striped8(idx):
    return np.concatenate([x.reshape(-1, 16).T for x in idx]).astype(np.uint16)


def runs(offs, k):
    lists = np.stack([offs[16 * r : 16 * r + 16].T.reshape(-1) for r in range(8)]).astype(np.int64)
    return lists[np.arange(k) % 512 // 64]


def pack_weight(w):
    k, n = w.shape
    w = f64(np.asarray(w, np.float32).astype(ml_dtypes.bfloat16)).reshape(k // 32, 32, n)
    amax = np.abs(w).max(1)
    byte = np.clip(np.where(amax > 0, np.frexp(amax)[1] - 1 + 127 - 7, 1), 1, 254)
    scaled = (w * np.exp2(127.0 - byte)[:, None, :]).reshape(k, n).astype(np.float32)
    words = np.ascontiguousarray(scaled.reshape(k // 512, 128, 4, n).transpose(0, 1, 3, 2)).astype(ml_dtypes.float8_e4m3fn).view(np.uint8)
    return words, np.ascontiguousarray(byte.astype(np.uint8).reshape(k // 512, 16, n))


def unpack_weight(words, scales):
    g, p, n, _ = words.shape
    vals = np.ascontiguousarray(words).view(ml_dtypes.float8_e4m3fn).astype(np.float64) * np.repeat(np.exp2(scales.astype(np.float64) - 127.0), 8, axis=1)[..., None]
    return vals.transpose(0, 1, 3, 2).reshape(g * 512, n)


E2M1 = np.array([0.0, 0.5, 1.0, 1.5, 2.0, 3.0, 4.0, 6.0, -0.0, -0.5, -1.0, -1.5, -2.0, -3.0, -4.0, -6.0])


def pack_fp4(w):
    k, n = w.shape
    w = f64(np.asarray(w, np.float32).astype(ml_dtypes.bfloat16)).reshape(k // 32, 32, n)
    amax = np.abs(w).max(1)
    mant, ex = np.frexp(amax / 6.0)
    byte = np.clip(np.where(amax > 0, np.where(mant > 0.5, ex, ex - 1) + 127, 1), 1, 254)
    scaled = (w * np.exp2(127.0 - byte)[:, None, :]).reshape(k, n).astype(np.float32)
    c = np.ascontiguousarray(scaled.reshape(k // 512, 128, 4, n).transpose(0, 1, 3, 2)).astype(ml_dtypes.float4_e2m1fn).view(np.uint8) & 0xF
    words = (c[..., 0::2] | (c[..., 1::2] << 4)).reshape(k // 512, 128, 2 * n)
    return np.ascontiguousarray(words), np.ascontiguousarray(byte.astype(np.uint8).reshape(k // 512, 16, n))


def unpack_fp4(words, scales):
    g, _, n = scales.shape
    words = np.ascontiguousarray(words).reshape(g, 128, n, 2)
    nib = np.empty((g, 128, n, 4), np.uint8)
    nib[..., 0::2] = words & 0xF
    nib[..., 1::2] = words >> 4
    vals = E2M1[nib] * np.repeat(np.exp2(scales.astype(np.float64) - 127.0), 8, axis=1)[..., None]
    return vals.transpose(0, 1, 3, 2).reshape(g * 512, n)


K, T, S, H, G, W = 512, 1024, 512, 512, 2048, 256


def setup_inputs():
    n = np.random.standard_normal
    s = mx_kscale(K)[:, None]
    packed_xT = pack_weight(n((K, T)) * s)
    packed_w1 = pack_fp4(n((K, H)) / np.sqrt(K) / s)
    packed_dT = pack_weight(n((K, G)) / s)
    perm = np.random.permutation(S)
    return {
        "x_words": packed_xT[0],
        "x_scales": packed_xT[1],
        "w1_words": packed_w1[0],
        "w1_scales": packed_w1[1],
        "gs": (np.random.uniform(0.5, 1.5, (K, 1)) * s).astype(np.float32),
        "d_words": packed_dT[0],
        "d_scales": packed_dT[1],
        "offs": striped(np.random.permutation(T)[:S]),
        "n1": striped8(np.stack([np.random.permutation(S) for _ in range(8)])),
        "n2": striped8(np.stack([np.random.permutation(S) for _ in range(8)])),
        "k1": striped8(np.random.randint(0, G, (8, H))),
        "k2": striped8(np.random.randint(0, G, (8, H))),
        "hz": striped8(np.random.randint(0, T, (8, S))),
        "n3": striped(perm[:W]),
        "n4": striped(perm[W:]),
    }


def reference(x_words, x_scales, w1_words, w1_scales, gs, d_words, d_scales, offs, n1, n2, k1, k2, hz, n3, n4):
    d_k1 = unpack_weight(d_words, d_scales)[np.arange(K)[:, None], runs(k1, K)]
    xq = unpack_weight(x_words, x_scales)[:, unstriped(offs)]
    y = unpack_fp4(w1_words, w1_scales).T @ xq
    ds = np.zeros((H, S))
    ds[np.arange(H)[:, None], runs(n1, H)] = y
    ds2 = np.zeros((H, S))
    ds2[np.arange(H)[:, None], runs(n2, H)] = y
    z = f64(gs) * np.maximum(ds, ds2)
    d_k2 = unpack_weight(d_words, d_scales)[np.arange(K)[:, None], runs(k2, K)]
    x_hz = unpack_weight(x_words, x_scales)[np.arange(K)[:, None], runs(hz, K)]
    h = 0.0625 * ((d_k1.T @ mxq(z, 0, "e4m3") + d_k2.T @ x_hz))
    pa = h[:, unstriped(n3)]
    pb = h[:, unstriped(n4)]
    ra = np.maximum(pa, pb)
    out = h.copy()
    out[:, unstriped(n3)] = ra
    return out

@@ -1,0 +1,214 @@
+from contextlib import ExitStack
+
+import concourse.mybir as mybir
+
+K, T, S, H, G, W = 512, 1024, 512, 512, 2048, 256
+FLOPS = 3 * 2 * K * H * S
+
+F32 = mybir.dt.float32
+BF16 = mybir.dt.bfloat16
+I32 = mybir.dt.int32
+U32 = mybir.dt.uint32
+U16 = mybir.dt.uint16
+U8 = mybir.dt.uint8
+FP8X4 = mybir.dt.float8_e4m3fn_x4
+FP4X4 = mybir.dt.float4_e2m1fn_x4
+COPY = mybir.ActivationFunctionType.Copy
+MAX = mybir.AluOpType.max
+MULT = mybir.AluOpType.mult
+
+P = 128
+PACK = 4
+HALF = S // 2
+
+
+def tile_picked_cmixhsendtwofill_none_p_kernel(
+    tc, x_words, x_scales, w1_words, w1_scales, gs, d_words, d_scales, offs, n1, n2, k1, k2, hz, n3, n4, out
+):
+    nc = tc.nc
+    with ExitStack() as ctx:
+        lists = ctx.enter_context(tc.tile_pool(name="lists", bufs=1))
+        sb = ctx.enter_context(tc.tile_pool(name="sb", bufs=1))
+        psum = ctx.enter_context(tc.psum_pool(name="psum", bufs=1))
+
+        def load_list(name, src):
+            tile = lists.tile(list(src.shape), U16, name=name)
+            nc.sync.dma_start(tile[:], src)
+            return tile
+
+        def zeroed_bytes(name, width):
+            tile = sb.tile([P, width], U8, name=name, align_bytes=64)
+            nc.vector.memset(tile[:].bitcast(I32), 0)
+            return tile
+
+        x_scale_table = zeroed_bytes("x_scale_table", T)
+        w1_scale_raw = zeroed_bytes("w1_scale_raw", H)
+        d_scale_table = zeroed_bytes("d_scale_table", G)
+        x_planes = zeroed_bytes("x_planes", 2 * S)
+        d_planes = zeroed_bytes("d_planes", 2 * H)
+
+        offs_l = load_list("offs_l", offs)
+        nc.scalar.dma_start(x_scale_table[0:P:8, :].bitcast(I32), x_scales[0].bitcast(I32))
+        hz_l = load_list("hz_l", hz)
+        x_table = sb.tile([P, T], U32, name="x_table", align_bytes=64)
+        nc.sync.dma_start(x_table[:].bitcast(I32), x_words[0].rearrange("p n t -> p (n t)").bitcast(I32))
+        for q in range(4):
+            nc.scalar.dma_start(
+                w1_scale_raw[32 * q : 32 * q + 4, :].bitcast(I32), w1_scales[0, 4 * q : 4 * q + 4, :].bitcast(I32)
+            )
+        w1_raw = sb.tile([P, 2 * H], U8, name="w1_raw", align_bytes=64)
+        nc.sync.dma_start(w1_raw[:].bitcast(I32), w1_words[0].bitcast(I32))
+        nc.scalar.dma_start(d_scale_table[0:P:8, :].bitcast(I32), d_scales[0].bitcast(I32))
+        k1_l = load_list("k1_l", k1)
+        k2_l = load_list("k2_l", k2)
+        n1_l = load_list("n1_l", n1)
+        n2_l = load_list("n2_l", n2)
+        d_table = sb.tile([P, G], U32, name="d_table", align_bytes=64)
+        nc.sync.dma_start(d_table[:].bitcast(I32), d_words[0].rearrange("p n t -> p (n t)").bitcast(I32))
+        gs_sb = sb.tile([P, PACK], F32, name="gs_sb")
+        nc.sync.dma_start(gs_sb[:], gs.rearrange("(p t) o -> p (t o)", t=PACK))
+        n3_l = load_list("n3_l", n3)
+        n4_l = load_list("n4_l", n4)
+
+        def picked_planes(name, table, first, second, planes):
+            picked = sb.tile([P, 2 * S], U8, name=name, align_bytes=64)
+            nc.vector.tensor_copy(picked[:, 0:S], table[:].indirect(first[:]))
+            nc.vector.tensor_copy(picked[:, S : 2 * S], table[:].indirect(second[:]))
+            for c in range(4):
+                nc.sync.dma_start(planes[c:P:32, :].bitcast(I32), picked[8 * c : P : 32, :].bitcast(I32))
+
+        def picked_words(name, table, offsets, tag):
+            picked = sb.tile([P, S], U32, name=name, tag=tag, align_bytes=64)
+            nc.vector.tensor_copy(picked[:], table[:].indirect(offsets[:]))
+            return picked
+
+        picked_planes("x_picked", x_scale_table, offs_l, hz_l, x_planes)
+
+        w1_plane = sb.tile([P, H], U8, name="w1_plane", align_bytes=64)
+        nc.vector.tensor_copy(
+            w1_plane[:].rearrange("p (t m) -> p t m", t=PACK), w1_scale_raw[:].rearrange("p (m t) -> p t m", t=PACK)
+        )
+        w1_dealt = sb.tile([P, 2 * H], U8, name="w1_dealt", align_bytes=64)
+        nc.scalar.copy(
+            w1_dealt[:].bitcast(U16).rearrange("p (t m) -> p t m", t=PACK),
+            w1_raw[:].bitcast(U16).rearrange("p (m t) -> p t m", t=PACK),
+        )
+        xq = picked_words("xq", x_table, offs_l, "xq")
+
+        y_sb = []
+        for t in range(PACK):
+            y_ps = psum.tile([P, S], F32, name=f"y_ps{t}")
+            nc.tensor.matmul_mx(
+                out=y_ps[:],
+                lhsT=w1_dealt[:, 2 * P * t : 2 * P * (t + 1)].bitcast(FP4X4),
+                lhsT_scale=w1_plane[:, P * t : P * (t + 1)],
+                rhs=xq[:].bitcast(FP8X4),
+                rhs_scale=x_planes[:, 0:S],
+                start=True,
+                stop=True,
+            )
+            y = sb.tile([P, S], F32, name=f"y{t}", tag=f"y{t}", align_bytes=64)
+            nc.scalar.copy(y[:], y_ps[:])
+            y_sb.append(y)
+
+        picked_planes("d_picked", d_scale_table, k1_l, k2_l, d_planes)
+        x_hz = picked_words("x_hz", x_table, hz_l, "x_hz")
+        d_k2 = picked_words("d_k2", d_table, k2_l, "d_k2")
+
+        h_ps = [psum.tile([P, S], F32, name=f"h_ps{i}") for i in range(4)]
+        for i in range(4):
+            nc.tensor.matmul_mx(
+                out=h_ps[i][:],
+                lhsT=d_k2[:, P * i : P * (i + 1)].bitcast(FP8X4),
+                lhsT_scale=d_planes[:, H + P * i : H + P * (i + 1)],
+                rhs=x_hz[:].bitcast(FP8X4),
+                rhs_scale=x_planes[:, S : 2 * S],
+                start=True,
+                stop=False,
+            )
+
+        z_bf = sb.tile([P, S, PACK], BF16, name="z_bf", align_bytes=64)
+        for t in range(PACK):
+            ds = sb.tile([P, 2 * S], F32, name=f"ds_{t}")
+            ds2 = sb.tile([P, 2 * S], F32, name=f"ds2_{t}")
+            nc.vector.tensor_copy(ds[:].indirect(n1_l[:]), y_sb[t][:])
+            nc.vector.tensor_copy(ds2[:].indirect(n2_l[:]), y_sb[t][:])
+            larger = sb.tile([P, S], F32, name=f"larger{t}")
+            pieces = [slice(0, S)] if t < PACK - 1 else [slice(0, HALF), slice(HALF, S)]
+            for cols in pieces:
+                nc.vector.tensor_tensor(larger[:, cols], ds[:, cols], ds2[:, cols], MAX)
+                nc.scalar.activation(z_bf[:, cols, t], larger[:, cols], COPY, scale=gs_sb[:, t : t + 1])
+
+        d_k1 = picked_words("d_k1", d_table, k1_l, f"y{PACK - 1}")
+
+        z_words = sb.tile([P, S], U32, name="z_words", align_bytes=64)
+        z_plane = sb.tile([P, S], U8, name="z_plane", align_bytes=64)
+        for cols in (slice(0, HALF), slice(HALF, S)):
+            nc.vector.quantize_mx(
+                out=z_words[:, cols].bitcast(FP8X4),
+                scales=z_plane[:, cols],
+                in_=z_bf[:, cols, :].rearrange("p j t -> p (j t)"),
+            )
+
+        def z_pass(i, cols, stop):
+            nc.tensor.matmul_mx(
+                out=h_ps[i][:, cols],
+                lhsT=d_k1[:, P * i : P * (i + 1)].bitcast(FP8X4),
+                lhsT_scale=d_planes[:, P * i : P * (i + 1)],
+                rhs=z_words[:, cols].bitcast(FP8X4),
+                rhs_scale=z_plane[:, cols],
+                start=False,
+                stop=stop,
+            )
+
+        for i in (0, 1):
+            z_pass(i, slice(0, HALF), False)
+        for i in (0, 1):
+            z_pass(i, slice(HALF, S), True)
+        for i in (2, 3):
+            z_pass(i, slice(0, S), True)
+
+        h = [sb.tile([P, S], F32, name=f"h{i}") for i in range(4)]
+        pa = [sb.tile([P, W], F32, name=f"pa{i}") for i in range(4)]
+        pb = [sb.tile([P, W], F32, name=f"pb{i}") for i in range(4)]
+        ra = [sb.tile([P, W], F32, name=f"ra{i}") for i in range(4)]
+
+        def leave_psum(i):
+            if i == 1:
+                nc.vector.tensor_scalar(h[i][:], h_ps[i][:], 0.0625, None, MULT)
+            else:
+                nc.scalar.activation(h[i][:], h_ps[i][:], COPY, scale=0.0625)
+
+        def move(i, dst, src):
+            if i % 2:
+                nc.vector.tensor_copy(dst, src)
+            else:
+                nc.scalar.activation(dst, src, COPY)
+
+        def fetch(i):
+            move(i, pa[i][:], h[i][:].indirect(n3_l[:]))
+            move(i, pb[i][:], h[i][:].indirect(n4_l[:]))
+
+        def pair_max(i):
+            nc.vector.tensor_tensor(ra[i][:], pa[i][:], pb[i][:], MAX)
+
+        def put(i):
+            move(i, h[i][:].indirect(n3_l[:]), ra[i][:])
+            nc.sync.dma_start(out[P * i : P * (i + 1), :], h[i][:])
+
+        leave_psum(0)
+        leave_psum(1)
+        fetch(0)
+        fetch(1)
+        leave_psum(2)
+        leave_psum(3)
+        pair_max(0)
+        pair_max(1)
+        put(0)
+        put(1)
+        fetch(2)
+        fetch(3)
+        pair_max(3)
+        pair_max(2)
+        put(2)
+        put(3)

@@ -14,6 +14,8 @@ U8 = mybir.dt.uint8
 FP8X4 = mybir.dt.float8_e4m3fn_x4
 FP4X4 = mybir.dt.float4_e2m1fn_x4
 COPY = mybir.ActivationFunctionType.Copy
+ABS = mybir.ActivationFunctionType.Abs
+SIGN = mybir.ActivationFunctionType.Sign
 MAX = mybir.AluOpType.max
 MULT = mybir.AluOpType.mult
 
@@ -41,14 +43,15 @@ def tile_picked_cmixhsendtwofill_none_p_kernel(
             nc.vector.memset(tile[:].bitcast(I32), 0)
             return tile
 
-        x_scale_table = zeroed_bytes("x_scale_table", T)
+        x_scale_table = sb.tile([P, T], U8, name="x_scale_table", align_bytes=64)
         w1_scale_raw = zeroed_bytes("w1_scale_raw", H)
         d_scale_table = zeroed_bytes("d_scale_table", G)
         x_planes = zeroed_bytes("x_planes", 2 * S)
-        d_planes = zeroed_bytes("d_planes", 2 * H)
 
         offs_l = load_list("offs_l", offs)
-        nc.scalar.dma_start(x_scale_table[0:P:8, :].bitcast(I32), x_scales[0].bitcast(I32))
+        nc.scalar.dma_start(
+            x_scale_table[:].bitcast(I32), x_scales[0].bitcast(I32).unsqueeze(1).broadcast_to([16, 8, T // 4])
+        )
         hz_l = load_list("hz_l", hz)
         x_table = sb.tile([P, T], U32, name="x_table", align_bytes=64)
         nc.sync.dma_start(x_table[:].bitcast(I32), x_words[0].rearrange("p n t -> p (n t)").bitcast(I32))
@@ -63,17 +66,20 @@ def tile_picked_cmixhsendtwofill_none_p_kernel(
         k2_l = load_list("k2_l", k2)
         n1_l = load_list("n1_l", n1)
         n2_l = load_list("n2_l", n2)
-        d_table = sb.tile([P, G], U32, name="d_table", align_bytes=64)
+        d_table = sb.tile([P, G], U32, name="d_table", tag="d_table", align_bytes=64)
         nc.sync.dma_start(d_table[:].bitcast(I32), d_words[0].rearrange("p n t -> p (n t)").bitcast(I32))
         gs_sb = sb.tile([P, PACK], F32, name="gs_sb")
         nc.sync.dma_start(gs_sb[:], gs.rearrange("(p t) o -> p (t o)", t=PACK))
         n3_l = load_list("n3_l", n3)
         n4_l = load_list("n4_l", n4)
 
-        def picked_planes(name, table, first, second, planes):
+        def picked_scales(name, table, first, second):
             picked = sb.tile([P, 2 * S], U8, name=name, align_bytes=64)
             nc.vector.tensor_copy(picked[:, 0:S], table[:].indirect(first[:]))
             nc.vector.tensor_copy(picked[:, S : 2 * S], table[:].indirect(second[:]))
+            return picked
+
+        def place_scales(planes, picked):
             for c in range(4):
                 nc.sync.dma_start(planes[c:P:32, :].bitcast(I32), picked[8 * c : P : 32, :].bitcast(I32))
 
@@ -82,7 +88,7 @@ def tile_picked_cmixhsendtwofill_none_p_kernel(
             nc.vector.tensor_copy(picked[:], table[:].indirect(offsets[:]))
             return picked
 
-        picked_planes("x_picked", x_scale_table, offs_l, hz_l, x_planes)
+        place_scales(x_planes, picked_scales("x_picked", x_scale_table, offs_l, hz_l))
 
         w1_plane = sb.tile([P, H], U8, name="w1_plane", align_bytes=64)
         nc.vector.tensor_copy(
@@ -97,7 +103,7 @@ def tile_picked_cmixhsendtwofill_none_p_kernel(
 
         y_sb = []
         for t in range(PACK):
-            y_ps = psum.tile([P, S], F32, name=f"y_ps{t}")
+            y_ps = psum.tile([P, S], F32, name=f"y_ps{t}", tag=f"y_ps{t}")
             nc.tensor.matmul_mx(
                 out=y_ps[:],
                 lhsT=w1_dealt[:, 2 * P * t : 2 * P * (t + 1)].bitcast(FP4X4),
@@ -111,104 +117,125 @@ def tile_picked_cmixhsendtwofill_none_p_kernel(
             nc.scalar.copy(y[:], y_ps[:])
             y_sb.append(y)
 
-        picked_planes("d_picked", d_scale_table, k1_l, k2_l, d_planes)
+        d_picked = picked_scales("d_picked", d_scale_table, k1_l, k2_l)
         x_hz = picked_words("x_hz", x_table, hz_l, "x_hz")
         d_k2 = picked_words("d_k2", d_table, k2_l, "d_k2")
 
-        h_ps = [psum.tile([P, S], F32, name=f"h_ps{i}") for i in range(4)]
-        for i in range(4):
-            nc.tensor.matmul_mx(
-                out=h_ps[i][:],
-                lhsT=d_k2[:, P * i : P * (i + 1)].bitcast(FP8X4),
-                lhsT_scale=d_planes[:, H + P * i : H + P * (i + 1)],
-                rhs=x_hz[:].bitcast(FP8X4),
-                rhs_scale=x_planes[:, S : 2 * S],
-                start=True,
-                stop=False,
-            )
+        halves = (slice(0, HALF), slice(HALF, S))
+        h_ps = [
+            [psum.tile([P, HALF], F32, name=f"h_ps{i}_0"), psum.tile([P, HALF], F32, name=f"h_ps{i}_1", tag=f"y_ps{i}")]
+            for i in range(4)
+        ]
 
-        z_bf = sb.tile([P, S, PACK], BF16, name="z_bf", align_bytes=64)
+        z_bf = [sb.tile([P, HALF, PACK], BF16, name=f"z_bf{u}", tag=f"z_bf{u}", align_bytes=64) for u in range(2)]
+        gs_abs = sb.tile([P, PACK], F32, name="gs_abs")
+        gs_sign = sb.tile([P, PACK], F32, name="gs_sign")
+        nc.scalar.activation(gs_abs[:], gs_sb[:], ABS)
+        nc.scalar.activation(gs_sign[:], gs_sb[:], SIGN)
         for t in range(PACK):
-            ds = sb.tile([P, 2 * S], F32, name=f"ds_{t}")
-            ds2 = sb.tile([P, 2 * S], F32, name=f"ds2_{t}")
+            ds = sb.tile([P, 2 * S], F32, name=f"ds_{t}", tag=f"larger{t - 2}", align_bytes=64)
+            ds2 = sb.tile([P, 2 * S], F32, name=f"ds2_{t}", tag="ds2", align_bytes=64)
             nc.vector.tensor_copy(ds[:].indirect(n1_l[:]), y_sb[t][:])
             nc.vector.tensor_copy(ds2[:].indirect(n2_l[:]), y_sb[t][:])
-            larger = sb.tile([P, S], F32, name=f"larger{t}")
-            pieces = [slice(0, S)] if t < PACK - 1 else [slice(0, HALF), slice(HALF, S)]
-            for cols in pieces:
-                nc.vector.tensor_tensor(larger[:, cols], ds[:, cols], ds2[:, cols], MAX)
-                nc.scalar.activation(z_bf[:, cols, t], larger[:, cols], COPY, scale=gs_sb[:, t : t + 1])
+            if t < PACK - 1:
+                a = sb.tile([P, S], BF16, name=f"a{t}", tag=f"a{t}", align_bytes=64)
+                b = sb.tile([P, S], BF16, name=f"b{t}")
+                larger = sb.tile([P, S], BF16, name=f"larger{t}", tag=f"larger{t}", align_bytes=64)
+                nc.scalar.activation(a[:], ds[:, 0:S], COPY, scale=gs_abs[:, t : t + 1])
+                nc.scalar.activation(b[:], ds2[:, 0:S], COPY, scale=gs_abs[:, t : t + 1])
+                nc.vector.tensor_tensor(larger[:], a[:], b[:], MAX)
+                factor = gs_sign
+            else:
+                larger = sb.tile([P, S], F32, name=f"larger{t}")
+                for cols in halves:
+                    nc.vector.tensor_tensor(larger[:, cols], ds[:, cols], ds2[:, cols], MAX)
+                factor = gs_sb
+            for u, cols in enumerate(halves):
+                nc.scalar.activation(z_bf[u][:, :, t], larger[:, cols], COPY, scale=factor[:, t : t + 1])
 
-        d_k1 = picked_words("d_k1", d_table, k1_l, f"y{PACK - 1}")
+        d_planes = sb.tile([P, 2 * H], U8, name="d_planes", tag=f"a{PACK - 2}", align_bytes=64)
+        nc.gpsimd.memset(d_planes[:].bitcast(I32), 0)
+        place_scales(d_planes, d_picked)
+        for u, cols in enumerate(halves):
+            for i in range(4):
+                nc.tensor.matmul_mx(
+                    out=h_ps[i][u][:],
+                    lhsT=d_k2[:, P * i : P * (i + 1)].bitcast(FP8X4),
+                    lhsT_scale=d_planes[:, H + P * i : H + P * (i + 1)],
+                    rhs=x_hz[:, cols].bitcast(FP8X4),
+                    rhs_scale=x_planes[:, S + HALF * u : S + HALF * (u + 1)],
+                    start=True,
+                    stop=False,
+                )
 
-        z_words = sb.tile([P, S], U32, name="z_words", align_bytes=64)
+
+        z_words = [
+            sb.tile([P, HALF], U32, name=f"z_words{u}", tag=("z_words0", "d_table")[u], align_bytes=64) for u in range(2)
+        ]
         z_plane = sb.tile([P, S], U8, name="z_plane", align_bytes=64)
-        for cols in (slice(0, HALF), slice(HALF, S)):
+        d_k1 = []
+        for u, cols in enumerate(halves):
+            picked = sb.tile([P, HALF], U32, name=f"d_k1_{u}", tag=(f"y{PACK - 1}", "z_bf0")[u], align_bytes=64)
+            nc.vector.tensor_copy(picked[:], d_table[:].indirect(k1_l[:, 16 * u : 16 * (u + 1)]))
+            d_k1.append(picked)
             nc.vector.quantize_mx(
-                out=z_words[:, cols].bitcast(FP8X4),
+                out=z_words[u][:].bitcast(FP8X4),
                 scales=z_plane[:, cols],
-                in_=z_bf[:, cols, :].rearrange("p j t -> p (j t)"),
+                in_=z_bf[u][:].rearrange("p j t -> p (j t)"),
             )
-
-        def z_pass(i, cols, stop):
-            nc.tensor.matmul_mx(
-                out=h_ps[i][:, cols],
-                lhsT=d_k1[:, P * i : P * (i + 1)].bitcast(FP8X4),
-                lhsT_scale=d_planes[:, P * i : P * (i + 1)],
-                rhs=z_words[:, cols].bitcast(FP8X4),
-                rhs_scale=z_plane[:, cols],
-                start=False,
-                stop=stop,
-            )
-
-        for i in (0, 1):
-            z_pass(i, slice(0, HALF), False)
-        for i in (0, 1):
-            z_pass(i, slice(HALF, S), True)
-        for i in (2, 3):
-            z_pass(i, slice(0, S), True)
 
         h = [sb.tile([P, S], F32, name=f"h{i}") for i in range(4)]
-        pa = [sb.tile([P, W], F32, name=f"pa{i}") for i in range(4)]
-        pb = [sb.tile([P, W], F32, name=f"pb{i}") for i in range(4)]
-        ra = [sb.tile([P, W], F32, name=f"ra{i}") for i in range(4)]
 
-        def leave_psum(i):
-            if i == 1:
-                nc.vector.tensor_scalar(h[i][:], h_ps[i][:], 0.0625, None, MULT)
+        def leave_psum(i, u):
+            if i == 1 or (i, u) in ((3, 0), (2, 1)):
+                nc.vector.tensor_scalar(h[i][:, halves[u]], h_ps[i][u][:], 0.0625, None, MULT)
             else:
-                nc.scalar.activation(h[i][:], h_ps[i][:], COPY, scale=0.0625)
+                nc.scalar.activation(h[i][:, halves[u]], h_ps[i][u][:], COPY, scale=0.0625)
 
-        def move(i, dst, src):
-            if i % 2:
+        for u, cols in enumerate(halves):
+            for i in (0, 1, 3, 2):
+                nc.tensor.matmul_mx(
+                    out=h_ps[i][u][:],
+                    lhsT=d_k1[i // 2][:, P * (i % 2) : P * (i % 2 + 1)].bitcast(FP8X4),
+                    lhsT_scale=d_planes[:, P * i : P * (i + 1)],
+                    rhs=z_words[u][:].bitcast(FP8X4),
+                    rhs_scale=z_plane[:, cols],
+                    start=False,
+                    stop=True,
+                )
+                leave_psum(i, u)
+
+        pa = [sb.tile([P, 2 * W], F32, name=f"pa{i}") for i in range(2)]
+        pb = [sb.tile([P, 2 * W], F32, name=f"pb{i}") for i in range(2)]
+        ra = [sb.tile([P, 2 * W], F32, name=f"ra{i}") for i in range(2)]
+
+        def move(on_vector, dst, src):
+            if on_vector:
                 nc.vector.tensor_copy(dst, src)
             else:
                 nc.scalar.activation(dst, src, COPY)
 
-        def fetch(i):
-            move(i, pa[i][:], h[i][:].indirect(n3_l[:]))
-            move(i, pb[i][:], h[i][:].indirect(n4_l[:]))
+        def part(tiles, i):
+            return tiles[i // 2][:, W * (i % 2) : W * (i % 2 + 1)]
 
-        def pair_max(i):
-            nc.vector.tensor_tensor(ra[i][:], pa[i][:], pb[i][:], MAX)
+        def fetch(i):
+            move(i % 2, part(pa, i), h[i][:].indirect(n3_l[:]))
+            move(i == 1, part(pb, i), h[i][:].indirect(n4_l[:]))
+
+        def pair_max(u):
+            nc.vector.tensor_tensor(ra[u][:], pa[u][:], pb[u][:], MAX)
 
         def put(i):
-            move(i, h[i][:].indirect(n3_l[:]), ra[i][:])
+            move(i % 2, h[i][:].indirect(n3_l[:]), part(ra, i))
             nc.sync.dma_start(out[P * i : P * (i + 1), :], h[i][:])
 
-        leave_psum(0)
-        leave_psum(1)
         fetch(0)
         fetch(1)
-        leave_psum(2)
-        leave_psum(3)
         pair_max(0)
-        pair_max(1)
-        put(0)
-        put(1)
         fetch(2)
         fetch(3)
-        pair_max(3)
-        pair_max(2)
+        put(0)
+        put(1)
+        pair_max(1)
         put(2)
         put(3)

@@ -43,7 +43,7 @@ def tile_picked_cmixhsendtwofill_none_p_kernel(
             nc.vector.memset(tile[:].bitcast(I32), 0)
             return tile
 
-        x_scale_table = sb.tile([P, T], U8, name="x_scale_table", align_bytes=64)
+        x_scale_table = sb.tile([P, T], U8, name="x_scale_table", tag="d_table", align_bytes=64)
         w1_scale_raw = zeroed_bytes("w1_scale_raw", H)
         d_scale_table = zeroed_bytes("d_scale_table", G)
         x_planes = zeroed_bytes("x_planes", 2 * S)
@@ -66,8 +66,6 @@ def tile_picked_cmixhsendtwofill_none_p_kernel(
         k2_l = load_list("k2_l", k2)
         n1_l = load_list("n1_l", n1)
         n2_l = load_list("n2_l", n2)
-        d_table = sb.tile([P, G], U32, name="d_table", tag="d_table", align_bytes=64)
-        nc.sync.dma_start(d_table[:].bitcast(I32), d_words[0].rearrange("p n t -> p (n t)").bitcast(I32))
         gs_sb = sb.tile([P, PACK], F32, name="gs_sb")
         nc.sync.dma_start(gs_sb[:], gs.rearrange("(p t) o -> p (t o)", t=PACK))
         n3_l = load_list("n3_l", n3)
@@ -89,6 +87,8 @@ def tile_picked_cmixhsendtwofill_none_p_kernel(
             return picked
 
         place_scales(x_planes, picked_scales("x_picked", x_scale_table, offs_l, hz_l))
+        d_table = sb.tile([P, G], U32, name="d_table", tag="d_table", align_bytes=64)
+        nc.sync.dma_start(d_table[:].bitcast(I32), d_words[0].rearrange("p n t -> p (n t)").bitcast(I32))
 
         w1_plane = sb.tile([P, H], U8, name="w1_plane", align_bytes=64)
         nc.vector.tensor_copy(
@@ -222,20 +222,21 @@ def tile_picked_cmixhsendtwofill_none_p_kernel(
             move(i % 2, part(pa, i), h[i][:].indirect(n3_l[:]))
             move(i == 1, part(pb, i), h[i][:].indirect(n4_l[:]))
 
-        def pair_max(u):
-            nc.vector.tensor_tensor(ra[u][:], pa[u][:], pb[u][:], MAX)
+        def pair_max(u, cols):
+            nc.vector.tensor_tensor(ra[u][:, cols], pa[u][:, cols], pb[u][:, cols], MAX)
 
         def put(i):
             move(i % 2, h[i][:].indirect(n3_l[:]), part(ra, i))
-            nc.sync.dma_start(out[P * i : P * (i + 1), :], h[i][:])
+            (nc.scalar if i == 2 else nc.sync).dma_start(out[P * i : P * (i + 1), :], h[i][:])
 
         fetch(0)
         fetch(1)
-        pair_max(0)
+        pair_max(0, slice(0, 2 * W))
         fetch(2)
         fetch(3)
+        pair_max(1, slice(0, W))
         put(0)
         put(1)
-        pair_max(1)
+        pair_max(1, slice(W, 2 * W))
         put(2)
         put(3)

@@ -21,7 +21,14 @@ MULT = mybir.AluOpType.mult
 
 P = 128
 PACK = 4
+QUADRANTS = 4
+QUADRANT = P // QUADRANTS
+BLOCKS = K // 32
+BLOCK_PARTS = P // BLOCKS
+H_TILES = H // P
 HALF = S // 2
+HALF_LIST = HALF // 16
+H_SCALE = 0.0625
 
 
 def tile_picked_cmixhsendtwofill_none_p_kernel(
@@ -50,18 +57,20 @@ def tile_picked_cmixhsendtwofill_none_p_kernel(
 
         offs_l = load_list("offs_l", offs)
         nc.scalar.dma_start(
-            x_scale_table[:].bitcast(I32), x_scales[0].bitcast(I32).unsqueeze(1).broadcast_to([16, 8, T // 4])
+            x_scale_table[:].bitcast(I32),
+            x_scales[0].bitcast(I32).unsqueeze(1).broadcast_to([BLOCKS, BLOCK_PARTS, T // 4]),
         )
         hz_l = load_list("hz_l", hz)
         x_table = sb.tile([P, T], U32, name="x_table", align_bytes=64)
         nc.sync.dma_start(x_table[:].bitcast(I32), x_words[0].rearrange("p n t -> p (n t)").bitcast(I32))
-        for q in range(4):
+        for q in range(QUADRANTS):
             nc.scalar.dma_start(
-                w1_scale_raw[32 * q : 32 * q + 4, :].bitcast(I32), w1_scales[0, 4 * q : 4 * q + 4, :].bitcast(I32)
+                w1_scale_raw[QUADRANT * q : QUADRANT * q + 4, :].bitcast(I32),
+                w1_scales[0, 4 * q : 4 * q + 4, :].bitcast(I32),
             )
         w1_raw = sb.tile([P, 2 * H], U8, name="w1_raw", align_bytes=64)
         nc.sync.dma_start(w1_raw[:].bitcast(I32), w1_words[0].bitcast(I32))
-        nc.scalar.dma_start(d_scale_table[0:P:8, :].bitcast(I32), d_scales[0].bitcast(I32))
+        nc.scalar.dma_start(d_scale_table[0:P:BLOCK_PARTS, :].bitcast(I32), d_scales[0].bitcast(I32))
         k1_l = load_list("k1_l", k1)
         k2_l = load_list("k2_l", k2)
         n1_l = load_list("n1_l", n1)
@@ -79,10 +88,12 @@ def tile_picked_cmixhsendtwofill_none_p_kernel(
 
         def place_scales(planes, picked):
             for c in range(4):
-                nc.sync.dma_start(planes[c:P:32, :].bitcast(I32), picked[8 * c : P : 32, :].bitcast(I32))
+                nc.sync.dma_start(
+                    planes[c:P:QUADRANT, :].bitcast(I32), picked[BLOCK_PARTS * c : P : QUADRANT, :].bitcast(I32)
+                )
 
-        def picked_words(name, table, offsets, tag):
-            picked = sb.tile([P, S], U32, name=name, tag=tag, align_bytes=64)
+        def picked_words(name, table, offsets):
+            picked = sb.tile([P, S], U32, name=name, align_bytes=64)
             nc.vector.tensor_copy(picked[:], table[:].indirect(offsets[:]))
             return picked
 
@@ -90,8 +101,11 @@ def tile_picked_cmixhsendtwofill_none_p_kernel(
         d_table = sb.tile([P, G], U32, name="d_table", tag="d_table", align_bytes=64)
         nc.sync.dma_start(d_table[:].bitcast(I32), d_words[0].rearrange("p n t -> p (n t)").bitcast(I32))
 
+        xq = picked_words("xq", x_table, offs_l)
+        x_hz = picked_words("x_hz", x_table, hz_l)
+
         w1_plane = sb.tile([P, H], U8, name="w1_plane", align_bytes=64)
-        nc.vector.tensor_copy(
+        nc.gpsimd.tensor_copy(
             w1_plane[:].rearrange("p (t m) -> p t m", t=PACK), w1_scale_raw[:].rearrange("p (m t) -> p t m", t=PACK)
         )
         w1_dealt = sb.tile([P, 2 * H], U8, name="w1_dealt", align_bytes=64)
@@ -99,7 +113,6 @@ def tile_picked_cmixhsendtwofill_none_p_kernel(
             w1_dealt[:].bitcast(U16).rearrange("p (t m) -> p t m", t=PACK),
             w1_raw[:].bitcast(U16).rearrange("p (m t) -> p t m", t=PACK),
         )
-        xq = picked_words("xq", x_table, offs_l, "xq")
 
         y_sb = []
         for t in range(PACK):
@@ -118,13 +131,12 @@ def tile_picked_cmixhsendtwofill_none_p_kernel(
             y_sb.append(y)
 
         d_picked = picked_scales("d_picked", d_scale_table, k1_l, k2_l)
-        x_hz = picked_words("x_hz", x_table, hz_l, "x_hz")
-        d_k2 = picked_words("d_k2", d_table, k2_l, "d_k2")
+        d_k2 = picked_words("d_k2", d_table, k2_l)
 
         halves = (slice(0, HALF), slice(HALF, S))
         h_ps = [
             [psum.tile([P, HALF], F32, name=f"h_ps{i}_0"), psum.tile([P, HALF], F32, name=f"h_ps{i}_1", tag=f"y_ps{i}")]
-            for i in range(4)
+            for i in range(H_TILES)
         ]
 
         z_bf = [sb.tile([P, HALF, PACK], BF16, name=f"z_bf{u}", tag=f"z_bf{u}", align_bytes=64) for u in range(2)]
@@ -157,7 +169,7 @@ def tile_picked_cmixhsendtwofill_none_p_kernel(
         nc.gpsimd.memset(d_planes[:].bitcast(I32), 0)
         place_scales(d_planes, d_picked)
         for u, cols in enumerate(halves):
-            for i in range(4):
+            for i in range(H_TILES):
                 nc.tensor.matmul_mx(
                     out=h_ps[i][u][:],
                     lhsT=d_k2[:, P * i : P * (i + 1)].bitcast(FP8X4),
@@ -168,29 +180,29 @@ def tile_picked_cmixhsendtwofill_none_p_kernel(
                     stop=False,
                 )
 
-
         z_words = [
             sb.tile([P, HALF], U32, name=f"z_words{u}", tag=("z_words0", "d_table")[u], align_bytes=64) for u in range(2)
         ]
         z_plane = sb.tile([P, S], U8, name="z_plane", align_bytes=64)
         d_k1 = []
         for u, cols in enumerate(halves):
-            picked = sb.tile([P, HALF], U32, name=f"d_k1_{u}", tag=(f"y{PACK - 1}", "z_bf0")[u], align_bytes=64)
-            nc.vector.tensor_copy(picked[:], d_table[:].indirect(k1_l[:, 16 * u : 16 * (u + 1)]))
-            d_k1.append(picked)
+            piece = sb.tile([P, HALF], U32, name=f"d_k1_{u}", tag=(f"y{PACK - 1}", "z_bf0")[u], align_bytes=64)
+            nc.vector.tensor_copy(piece[:], d_table[:].indirect(k1_l[:, HALF_LIST * u : HALF_LIST * (u + 1)]))
+            d_k1.append(piece)
             nc.vector.quantize_mx(
                 out=z_words[u][:].bitcast(FP8X4),
                 scales=z_plane[:, cols],
                 in_=z_bf[u][:].rearrange("p j t -> p (j t)"),
             )
 
-        h = [sb.tile([P, S], F32, name=f"h{i}") for i in range(4)]
+        h = [sb.tile([P, S], F32, name=f"h{i}") for i in range(H_TILES)]
+        leaves_on_vector = ((1, 0), (3, 0), (1, 1), (2, 1))
 
         def leave_psum(i, u):
-            if i == 1 or (i, u) in ((3, 0), (2, 1)):
-                nc.vector.tensor_scalar(h[i][:, halves[u]], h_ps[i][u][:], 0.0625, None, MULT)
+            if (i, u) in leaves_on_vector:
+                nc.vector.tensor_scalar(h[i][:, halves[u]], h_ps[i][u][:], H_SCALE, None, MULT)
             else:
-                nc.scalar.activation(h[i][:, halves[u]], h_ps[i][u][:], COPY, scale=0.0625)
+                nc.scalar.activation(h[i][:, halves[u]], h_ps[i][u][:], COPY, scale=H_SCALE)
 
         for u, cols in enumerate(halves):
             for i in (0, 1, 3, 2):
@@ -205,9 +217,9 @@ def tile_picked_cmixhsendtwofill_none_p_kernel(
                 )
                 leave_psum(i, u)
 
-        pa = [sb.tile([P, 2 * W], F32, name=f"pa{i}") for i in range(2)]
-        pb = [sb.tile([P, 2 * W], F32, name=f"pb{i}") for i in range(2)]
-        ra = [sb.tile([P, 2 * W], F32, name=f"ra{i}") for i in range(2)]
+        pa = [sb.tile([P, 2 * W], F32, name=f"pa{pair}") for pair in range(2)]
+        pb = [sb.tile([P, 2 * W], F32, name=f"pb{pair}") for pair in range(2)]
+        ra = [sb.tile([P, 2 * W], F32, name=f"ra{pair}") for pair in range(2)]
 
         def move(on_vector, dst, src):
             if on_vector:
@@ -222,8 +234,8 @@ def tile_picked_cmixhsendtwofill_none_p_kernel(
             move(i % 2, part(pa, i), h[i][:].indirect(n3_l[:]))
             move(i == 1, part(pb, i), h[i][:].indirect(n4_l[:]))
 
-        def pair_max(u, cols):
-            nc.vector.tensor_tensor(ra[u][:, cols], pa[u][:, cols], pb[u][:, cols], MAX)
+        def pair_max(pair, cols):
+            nc.vector.tensor_tensor(ra[pair][:, cols], pa[pair][:, cols], pb[pair][:, cols], MAX)
 
         def put(i):
             move(i % 2, h[i][:].indirect(n3_l[:]), part(ra, i))

from contextlib import ExitStack

import concourse.mybir as mybir

K, T, S, H, G, W = 512, 1024, 512, 512, 2048, 256
FLOPS = 3 * 2 * K * H * S

F32 = mybir.dt.float32
BF16 = mybir.dt.bfloat16
I32 = mybir.dt.int32
U32 = mybir.dt.uint32
U16 = mybir.dt.uint16
U8 = mybir.dt.uint8
FP8X4 = mybir.dt.float8_e4m3fn_x4
FP4X4 = mybir.dt.float4_e2m1fn_x4
COPY = mybir.ActivationFunctionType.Copy
ABS = mybir.ActivationFunctionType.Abs
SIGN = mybir.ActivationFunctionType.Sign
MAX = mybir.AluOpType.max
MULT = mybir.AluOpType.mult

P = 128
PACK = 4
QUADRANTS = 4
QUADRANT = P // QUADRANTS
BLOCKS = K // 32
BLOCK_PARTS = P // BLOCKS
H_TILES = H // P
HALF = S // 2
HALF_LIST = HALF // 16
H_SCALE = 0.0625


def tile_picked_cmixhsendtwofill_none_p_kernel(
    tc, x_words, x_scales, w1_words, w1_scales, gs, d_words, d_scales, offs, n1, n2, k1, k2, hz, n3, n4, out
):
    nc = tc.nc
    with ExitStack() as ctx:
        lists = ctx.enter_context(tc.tile_pool(name="lists", bufs=1))
        sb = ctx.enter_context(tc.tile_pool(name="sb", bufs=1))
        psum = ctx.enter_context(tc.psum_pool(name="psum", bufs=1))

        def load_list(name, src):
            tile = lists.tile(list(src.shape), U16, name=name)
            nc.sync.dma_start(tile[:], src)
            return tile

        def zeroed_bytes(name, width):
            tile = sb.tile([P, width], U8, name=name, align_bytes=64)
            nc.vector.memset(tile[:].bitcast(I32), 0)
            return tile

        x_scale_table = sb.tile([P, T], U8, name="x_scale_table", tag="d_table", align_bytes=64)
        w1_scale_raw = zeroed_bytes("w1_scale_raw", H)
        d_scale_table = zeroed_bytes("d_scale_table", G)
        x_planes = zeroed_bytes("x_planes", 2 * S)

        offs_l = load_list("offs_l", offs)
        nc.scalar.dma_start(
            x_scale_table[:].bitcast(I32),
            x_scales[0].bitcast(I32).unsqueeze(1).broadcast_to([BLOCKS, BLOCK_PARTS, T // 4]),
        )
        hz_l = load_list("hz_l", hz)
        x_table = sb.tile([P, T], U32, name="x_table", align_bytes=64)
        nc.sync.dma_start(x_table[:].bitcast(I32), x_words[0].rearrange("p n t -> p (n t)").bitcast(I32))
        for q in range(QUADRANTS):
            nc.scalar.dma_start(
                w1_scale_raw[QUADRANT * q : QUADRANT * q + 4, :].bitcast(I32),
                w1_scales[0, 4 * q : 4 * q + 4, :].bitcast(I32),
            )
        w1_raw = sb.tile([P, 2 * H], U8, name="w1_raw", align_bytes=64)
        nc.sync.dma_start(w1_raw[:].bitcast(I32), w1_words[0].bitcast(I32))
        nc.scalar.dma_start(d_scale_table[0:P:BLOCK_PARTS, :].bitcast(I32), d_scales[0].bitcast(I32))
        k1_l = load_list("k1_l", k1)
        k2_l = load_list("k2_l", k2)
        n1_l = load_list("n1_l", n1)
        n2_l = load_list("n2_l", n2)
        gs_sb = sb.tile([P, PACK], F32, name="gs_sb")
        nc.sync.dma_start(gs_sb[:], gs.rearrange("(p t) o -> p (t o)", t=PACK))
        n3_l = load_list("n3_l", n3)
        n4_l = load_list("n4_l", n4)

        def picked_scales(name, table, first, second):
            picked = sb.tile([P, 2 * S], U8, name=name, align_bytes=64)
            nc.vector.tensor_copy(picked[:, 0:S], table[:].indirect(first[:]))
            nc.vector.tensor_copy(picked[:, S : 2 * S], table[:].indirect(second[:]))
            return picked

        def place_scales(planes, picked):
            for c in range(4):
                nc.sync.dma_start(
                    planes[c:P:QUADRANT, :].bitcast(I32), picked[BLOCK_PARTS * c : P : QUADRANT, :].bitcast(I32)
                )

        def picked_words(name, table, offsets):
            picked = sb.tile([P, S], U32, name=name, align_bytes=64)
            nc.vector.tensor_copy(picked[:], table[:].indirect(offsets[:]))
            return picked

        place_scales(x_planes, picked_scales("x_picked", x_scale_table, offs_l, hz_l))
        d_table = sb.tile([P, G], U32, name="d_table", tag="d_table", align_bytes=64)
        nc.sync.dma_start(d_table[:].bitcast(I32), d_words[0].rearrange("p n t -> p (n t)").bitcast(I32))

        xq = picked_words("xq", x_table, offs_l)
        x_hz = picked_words("x_hz", x_table, hz_l)

        w1_plane = sb.tile([P, H], U8, name="w1_plane", align_bytes=64)
        nc.gpsimd.tensor_copy(
            w1_plane[:].rearrange("p (t m) -> p t m", t=PACK), w1_scale_raw[:].rearrange("p (m t) -> p t m", t=PACK)
        )
        w1_dealt = sb.tile([P, 2 * H], U8, name="w1_dealt", align_bytes=64)
        nc.scalar.copy(
            w1_dealt[:].bitcast(U16).rearrange("p (t m) -> p t m", t=PACK),
            w1_raw[:].bitcast(U16).rearrange("p (m t) -> p t m", t=PACK),
        )

        y_sb = []
        for t in range(PACK):
            y_ps = psum.tile([P, S], F32, name=f"y_ps{t}", tag=f"y_ps{t}")
            nc.tensor.matmul_mx(
                out=y_ps[:],
                lhsT=w1_dealt[:, 2 * P * t : 2 * P * (t + 1)].bitcast(FP4X4),
                lhsT_scale=w1_plane[:, P * t : P * (t + 1)],
                rhs=xq[:].bitcast(FP8X4),
                rhs_scale=x_planes[:, 0:S],
                start=True,
                stop=True,
            )
            y = sb.tile([P, S], F32, name=f"y{t}", tag=f"y{t}", align_bytes=64)
            nc.scalar.copy(y[:], y_ps[:])
            y_sb.append(y)

        d_picked = picked_scales("d_picked", d_scale_table, k1_l, k2_l)
        d_k2 = picked_words("d_k2", d_table, k2_l)

        halves = (slice(0, HALF), slice(HALF, S))
        h_ps = [
            [psum.tile([P, HALF], F32, name=f"h_ps{i}_0"), psum.tile([P, HALF], F32, name=f"h_ps{i}_1", tag=f"y_ps{i}")]
            for i in range(H_TILES)
        ]

        z_bf = [sb.tile([P, HALF, PACK], BF16, name=f"z_bf{u}", tag=f"z_bf{u}", align_bytes=64) for u in range(2)]
        gs_abs = sb.tile([P, PACK], F32, name="gs_abs")
        gs_sign = sb.tile([P, PACK], F32, name="gs_sign")
        nc.scalar.activation(gs_abs[:], gs_sb[:], ABS)
        nc.scalar.activation(gs_sign[:], gs_sb[:], SIGN)
        for t in range(PACK):
            ds = sb.tile([P, 2 * S], F32, name=f"ds_{t}", tag=f"larger{t - 2}", align_bytes=64)
            ds2 = sb.tile([P, 2 * S], F32, name=f"ds2_{t}", tag="ds2", align_bytes=64)
            nc.vector.tensor_copy(ds[:].indirect(n1_l[:]), y_sb[t][:])
            nc.vector.tensor_copy(ds2[:].indirect(n2_l[:]), y_sb[t][:])
            if t < PACK - 1:
                a = sb.tile([P, S], BF16, name=f"a{t}", tag=f"a{t}", align_bytes=64)
                b = sb.tile([P, S], BF16, name=f"b{t}")
                larger = sb.tile([P, S], BF16, name=f"larger{t}", tag=f"larger{t}", align_bytes=64)
                nc.scalar.activation(a[:], ds[:, 0:S], COPY, scale=gs_abs[:, t : t + 1])
                nc.scalar.activation(b[:], ds2[:, 0:S], COPY, scale=gs_abs[:, t : t + 1])
                nc.vector.tensor_tensor(larger[:], a[:], b[:], MAX)
                factor = gs_sign
            else:
                larger = sb.tile([P, S], F32, name=f"larger{t}")
                for cols in halves:
                    nc.vector.tensor_tensor(larger[:, cols], ds[:, cols], ds2[:, cols], MAX)
                factor = gs_sb
            for u, cols in enumerate(halves):
                nc.scalar.activation(z_bf[u][:, :, t], larger[:, cols], COPY, scale=factor[:, t : t + 1])

        d_planes = sb.tile([P, 2 * H], U8, name="d_planes", tag=f"a{PACK - 2}", align_bytes=64)
        nc.gpsimd.memset(d_planes[:].bitcast(I32), 0)
        place_scales(d_planes, d_picked)
        for u, cols in enumerate(halves):
            for i in range(H_TILES):
                nc.tensor.matmul_mx(
                    out=h_ps[i][u][:],
                    lhsT=d_k2[:, P * i : P * (i + 1)].bitcast(FP8X4),
                    lhsT_scale=d_planes[:, H + P * i : H + P * (i + 1)],
                    rhs=x_hz[:, cols].bitcast(FP8X4),
                    rhs_scale=x_planes[:, S + HALF * u : S + HALF * (u + 1)],
                    start=True,
                    stop=False,
                )

        z_words = [
            sb.tile([P, HALF], U32, name=f"z_words{u}", tag=("z_words0", "d_table")[u], align_bytes=64) for u in range(2)
        ]
        z_plane = sb.tile([P, S], U8, name="z_plane", align_bytes=64)
        d_k1 = []
        for u, cols in enumerate(halves):
            piece = sb.tile([P, HALF], U32, name=f"d_k1_{u}", tag=(f"y{PACK - 1}", "z_bf0")[u], align_bytes=64)
            nc.vector.tensor_copy(piece[:], d_table[:].indirect(k1_l[:, HALF_LIST * u : HALF_LIST * (u + 1)]))
            d_k1.append(piece)
            nc.vector.quantize_mx(
                out=z_words[u][:].bitcast(FP8X4),
                scales=z_plane[:, cols],
                in_=z_bf[u][:].rearrange("p j t -> p (j t)"),
            )

        h = [sb.tile([P, S], F32, name=f"h{i}") for i in range(H_TILES)]
        leaves_on_vector = ((1, 0), (3, 0), (1, 1), (2, 1))

        def leave_psum(i, u):
            if (i, u) in leaves_on_vector:
                nc.vector.tensor_scalar(h[i][:, halves[u]], h_ps[i][u][:], H_SCALE, None, MULT)
            else:
                nc.scalar.activation(h[i][:, halves[u]], h_ps[i][u][:], COPY, scale=H_SCALE)

        for u, cols in enumerate(halves):
            for i in (0, 1, 3, 2):
                nc.tensor.matmul_mx(
                    out=h_ps[i][u][:],
                    lhsT=d_k1[i // 2][:, P * (i % 2) : P * (i % 2 + 1)].bitcast(FP8X4),
                    lhsT_scale=d_planes[:, P * i : P * (i + 1)],
                    rhs=z_words[u][:].bitcast(FP8X4),
                    rhs_scale=z_plane[:, cols],
                    start=False,
                    stop=True,
                )
                leave_psum(i, u)

        pa = [sb.tile([P, 2 * W], F32, name=f"pa{pair}") for pair in range(2)]
        pb = [sb.tile([P, 2 * W], F32, name=f"pb{pair}") for pair in range(2)]
        ra = [sb.tile([P, 2 * W], F32, name=f"ra{pair}") for pair in range(2)]

        def move(on_vector, dst, src):
            if on_vector:
                nc.vector.tensor_copy(dst, src)
            else:
                nc.scalar.activation(dst, src, COPY)

        def part(tiles, i):
            return tiles[i // 2][:, W * (i % 2) : W * (i % 2 + 1)]

        def fetch(i):
            move(i % 2, part(pa, i), h[i][:].indirect(n3_l[:]))
            move(i == 1, part(pb, i), h[i][:].indirect(n4_l[:]))

        def pair_max(pair, cols):
            nc.vector.tensor_tensor(ra[pair][:, cols], pa[pair][:, cols], pb[pair][:, cols], MAX)

        def put(i):
            move(i % 2, h[i][:].indirect(n3_l[:]), part(ra, i))
            (nc.scalar if i == 2 else nc.sync).dma_start(out[P * i : P * (i + 1), :], h[i][:])

        fetch(0)
        fetch(1)
        pair_max(0, slice(0, 2 * W))
        fetch(2)
        fetch(3)
        pair_max(1, slice(0, W))
        put(0)
        put(1)
        pair_max(1, slice(W, 2 * W))
        put(2)
        put(3)
